import numpy as np, ml_dtypes
CORES = [10,34,74,98]
N = 4
import mx_ref
BF = ml_dtypes.bfloat16
def entries(a):
    return np.ascontiguousarray(a.T).reshape(-1)
def table(e):
    return np.ascontiguousarray(np.reshape(e, (-1, 16)).T).astype(np.int32)
def cols(t, e):
    v = np.concatenate([t.reshape(128, -1, 4), np.zeros((128, 1, 4), BF)], axis=1)
    return np.ascontiguousarray(v[:, e]).reshape(128, -1)
def f(rng, *shape):
    return mx_ref.flush((rng.standard_normal(shape, dtype=np.float32) * np.exp2(rng.integers(-2, 3, shape[:-1] + (1,)))).astype(BF))
def wide(rng, *shape, cols=0):
    v = rng.standard_normal(shape, dtype=np.float32) * np.exp2(rng.integers(-12, 13, shape)).astype(np.float32)
    if cols: v *= np.repeat(np.exp2(rng.integers(-cols, cols + 1, shape[:-2] + (1, shape[-1] // 4))) * (rng.random(shape[:-2] + (1, shape[-1] // 4)) > 0.0625), 4, axis=-1).astype(np.float32)
    return mx_ref.flush(v.astype(BF))
T, S, CAPP = 1024, 256, 96
def lists(rng, most=None, own=False, share=False, edge=False):
    o, c, m = [], [], []
    for r in range(N):
        n = np.zeros(N, int)
        if own: n[r] = CAPP
        if most is not None:
            for q in rng.permutation(N)[:most]: n[q] = CAPP
            n = np.minimum(n, np.maximum(0, S - (np.cumsum(n) - n)))
        while n.sum() < S:
            q = rng.integers(0, N)
            if n[q] < CAPP: n[q] += 1
        slots = np.full(N * CAPP, -1); used = []
        for q in range(N):
            k = q * CAPP + rng.permutation(CAPP)[:n[q]]; used += list(k)
            slots[k] = rng.integers(0, T) if share else rng.choice([0, T - 1], n[q]) if edge else rng.integers(0, T, n[q])
        o.append(table(rng.choice([0, T - 1], S) if edge else rng.integers(0, T, S))); c.append(table(slots)); m.append(table(rng.permutation(used)))
    return {"own": np.stack(o), "want": np.stack(c), "slot": np.stack(m)}
def setup_inputs(rng):
    return {"x": f(rng, N, 128, 4 * T), "w": f(rng, N, 128, 512), **lists(rng)}
def setup_inputs_edge(rng):
    return {**setup_inputs(rng), **lists(rng, edge=True)}
def setup_inputs_full(rng):
    return {**setup_inputs(rng), **lists(rng, most=S // CAPP)}
def setup_inputs_self(rng):
    return {**setup_inputs(rng), **lists(rng, own=True)}
def setup_inputs_share(rng):
    return {**setup_inputs(rng), **lists(rng, share=True)}
def setup_inputs_spread(rng):
    d = setup_inputs(rng); d["x"] = wide(rng, N, 128, 4 * T, cols=8); return d
def check_inputs(d):
    b = []
    for r in range(N):
        o, c, m = entries(d["own"][r]), entries(d["want"][r]), entries(d["slot"][r])
        if o.min() < 0 or o.max() >= T: b.append("own")
        if c.min() < -1 or c.max() >= T: b.append("want")
        if m.min() < 0 or m.max() >= N * CAPP or len(set(m.tolist())) != S or (c[m] < 0).any() or (c >= 0).sum() != S: b.append("slot")
    return b
def decode(q):
    out = np.zeros(q[0].shape, np.float32)
    for b in range(4):
        e = np.zeros((128, 128, 4), np.float32); e[np.arange(128), np.arange(128), b] = 1
        out[:, b::4] = mx_ref.matmul(mx_ref.quantize(e.reshape(128, 512).astype(BF)), q)
    return out
def reference(x, w, own, want, slot):
    M = []
    for r in range(N):
        c = entries(want[r])
        arrived = np.concatenate([decode(mx_ref.quantize(cols(x[q], c[q * CAPP:(q + 1) * CAPP]))) for q in range(N)], axis=1)
        far = arrived.reshape(128, -1, 4)[:, entries(slot[r])].reshape(128, -1)
        M.append(mx_ref.quantize(((cols(x[r], entries(own[r])).astype(np.float32) + far) * np.float32(0.5)).astype(BF)))
    y = np.zeros((N, 128, 3 * S), np.float32)
    for r in range(N):
        for i in range(3): y[r][:, S * i:S * i + S] = mx_ref.matmul(mx_ref.quantize(w[r]), M[(r - 1 + i) % N])
    return {"y": y}

@@ -1,0 +1,286 @@
+from concourse.bass import DstId, RemoteDMATransfer
+from concourse.mybir import dt, AluOpType, ActivationFunctionType
+
+N, S, CAPP, R = 4, 256, 96, 1024
+SLOTS = N * CAPP
+PAD = 128 - CAPP
+F8 = "float8_e4m3fn_x4"
+L_OPP, L_PREV, L_SELF, L_NEXT, L_ALL = 0, CAPP, 2 * CAPP, 3 * CAPP + PAD, 4 * CAPP + PAD
+M_ALL = SLOTS + PAD
+
+SCRATCH = {
+    "xs": ("sbuf", [128, 4 * R], "bfloat16"),
+    "ws": ("sbuf", [128, 512], "bfloat16"),
+    "wl": ("sbuf", [128, 24], "int32"), "sl": ("sbuf", [128, 16], "int32"), "ol": ("sbuf", [128, 256], "int32"),
+    "w16": ("sbuf", [128, 24], "uint16"),
+    "lopp": ("sbuf", [128, 6], "uint16"), "lnext": ("sbuf", [128, 6], "uint16"), "lprev": ("sbuf", [128, 6], "uint16"),
+    "u1": ("sbuf", [128, 16], "int32"), "u2": ("sbuf", [128, 16], "int32"), "u3": ("sbuf", [128, 16], "int32"),
+    "pos16": ("sbuf", [128, 16], "uint16"), "pprev": ("sbuf", [128, 16], "uint16"), "pnext": ("sbuf", [128, 16], "uint16"),
+    "so": ("sbuf", [128, 32], "float32"), "sot": ("sbuf", [128, 32], "float32"), "so16": ("sbuf", [128, 16], "uint16"),
+    "flat": ("sbuf", [128, SLOTS], "float32"), "ownf": ("sbuf", [128, 24], "float32"), "own16": ("sbuf", [128, 24], "uint16"),
+    "half": ("sbuf", [128, 512], "bfloat16"), "ident": ("sbuf", [128, 128], "bfloat16"),
+    "et": ("sbuf", [128, 2048], "bfloat16"), "ec": ("sbuf", [128, 512], F8), "ep": ("sbuf", [128, 512], "uint8"),
+    "wc": ("sbuf", [128, 128], F8), "wp": ("sbuf", [128, 128], "uint8"),
+    "tself": ("sbuf", [128, 512], "bfloat16"),
+    "lc": ("sbuf", [128, L_ALL], F8), "lp": ("sbuf", [128, L_ALL], "uint8"),
+    "mc": ("sbuf", [128, M_ALL], F8), "mp": ("sbuf", [128, M_ALL], "uint8"),
+    "prevc": ("sbuf", [128, SLOTS], F8), "prevp": ("sbuf", [128, SLOTS], "uint8"),
+    "nextc": ("sbuf", [128, SLOTS], F8), "nextp": ("sbuf", [128, SLOTS], "uint8"),
+}
+for _k in ("next", "prev", "opp"):
+    SCRATCH["t" + _k] = ("sbuf", [128, 512], "bfloat16")
+    SCRATCH["c" + _k] = ("sbuf", [128, 128], F8)
+    SCRATCH["s" + _k] = ("sbuf", [128, 128], "uint8")
+for _k in range(2):
+    SCRATCH["xh%d" % _k] = ("sbuf", [128, 8 * CAPP], "bfloat16")
+for _k in range(4):
+    SCRATCH["mt%d" % _k] = ("sbuf", [128, 512], "bfloat16")
+for _k in range(3):
+    SCRATCH["yw%d" % _k] = ("sbuf", [128, SLOTS], "float32")
+    SCRATCH["ys%d" % _k] = ("sbuf", [128, S], "float32")
+for _k in range(8):
+    SCRATCH["ps%d" % _k] = ("psum", [128, 512], "float32")
+ARR = ["sent", "l_opp", "l_next", "l_prev", "p_next", "p_prev", "f_opp", "f_next", "f_prev",
+       "m_next0", "m_next1", "m_next2", "m_next3", "m_nextp", "m_prev0", "m_prev1", "m_prev2", "m_prev3", "m_prevp"]
+SEMAPHORES = ARR + ["e%d" % _k for _k in range(130)]
+
+
+def rank_program(g, core, T, topo):
+    r = T.rank_of(core)
+    if r is None:
+        return
+    V, A, PE, SY = g.vector, g.scalar, g.tensor, g.sync
+    queues = {"g": g, "V": V, "A": A, "PE": PE, "SY": SY}
+    add, mult = AluOpType.add, AluOpType.mult
+    COPY = ActivationFunctionType.Copy
+    nxt, prv, opp = (r + 1) % N, (r - 1) % N, (r + 2) % N
+    nevents = [0]
+    seen = set()
+    unwaited = {}
+
+    def event(n=1):
+        name = "e%d" % nevents[0]
+        nevents[0] += 1
+        unwaited[name] = n
+        return (name, n)
+
+    def wait(q, *evs):
+        for name, n in evs:
+            if (q, name) not in seen:
+                seen.add((q, name))
+                unwaited.pop(name, None)
+                queues[q].wait_ge(T.sem[name], n)
+
+    def done(ins, n=1):
+        e = event(n)
+        ins.then_inc(T.sem[e[0]], n)
+        return e
+
+    sent = [0]
+
+    def engs(k):
+        return topo.engines(core, T.cores[k])
+
+    def send(k, out, src, sem):
+        rid, pid, _ = topo.addr(T.cores[k])
+        g.remote_dma(out_ap=out, in_ap=src, remote_sem=T.sem[sem], local_sem=T.sem.sent, pid=pid, routing_id=rid,
+                     dma_engine_mask=topo.mask(core, T.cores[k]))
+        sent[0] += len(engs(k))
+
+    def send_two(items):
+        tr = []
+        for i, (k, out, src, sem) in enumerate(items):
+            es = engs(k)
+            es = es[i * len(es) // 2:(i + 1) * len(es) // 2]
+            sent[0] += len(es)
+            rid, pid, _ = topo.addr(T.cores[k])
+            tr.append(RemoteDMATransfer(dst_ids=[DstId(rid=rid, pnc=pid)], dma_engine_mask=sum(1 << e for e in es),
+                                        remote_sem=T.sem[sem], srcs=[src], dsts=[out]))
+        g.remote_dma_fused(tr, local_sem=T.sem.sent)
+
+    ne = len(engs(opp))
+    nh = ne // 2
+
+    def u8(v):
+        return v.bitcast(dt.uint8)
+
+    e_want, e_slot, e_own, e_x, e_w, e_of, e_y = (event(128), event(128), event(16), event(16), event(16), event(128), event(80))
+
+    def load(q, out, src, e):
+        q.dma_start(out, src).then_inc(T.sem[e[0]], 16)
+
+    for k in range(4):
+        load(SY, T.wl[16 * k:16 * k + 16, :], T.want[:], e_want)
+        load(A, T.wl[16 * k + 64:16 * k + 80, :], T.want[:], e_want)
+    for k in range(4):
+        load(SY, T.sl[16 * k:16 * k + 16, :], T.slot[:], e_slot)
+        load(A, T.sl[16 * k + 64:16 * k + 80, :], T.slot[:], e_slot)
+    load(SY, T.xs[:], T.x[:], e_x)
+
+    v_ol = done(V.memset(T.ol[:], 0))
+    v_half = done(V.memset(T.half[:], 0.5))
+    v_pad = {k: done(V.memset(T["t" + k][:, 4 * CAPP:512], 0.0)) for k in ("next", "prev", "opp", "self")}
+    v_mpad = [done(V.memset(T["mt%d" % i][:, 4 * CAPP:512], 0.0)) for i in range(4)]
+    z = [done(V.memset(T.et[:, 512 * b:512 * b + 512], 0.0)) for b in (0, 1)]
+    wait("A", v_ol)
+    load(A, T.ol[0:1, :], T.own[:], e_own)
+    load(A, T.ws[:], T.w[:], e_w)
+    wait("g", v_half)
+    g_id = done(g.affine_select(T.ident[:], T.half[:, 0:128], [[-1, 128]], AluOpType.is_equal, 0.0, 0, 1))
+    wait("A", v_half)
+    a_flat = done(A.activation(T.flat[:], T.half[:, 0:SLOTS], COPY, scale=0.0))
+    z += [done(A.activation(T.et[:, 512 * b:512 * b + 512], T.half[:], COPY, scale=0.0)) for b in (2, 3)]
+    wait("A", g_id)
+    a_e = []
+    for b in range(4):
+        wait("A", z[b])
+        a_e.append(done(A.activation(T.et[:, 512 * b + b:512 * b + 512:4], T.ident[:], COPY)))
+
+    wait("V", e_want)
+    v_w16 = done(V.tensor_scalar(T.w16[:], T.wl[:], 0, 4, AluOpType.max, mult))
+    wait("g", v_w16)
+
+    def wcols(k):
+        return T.w16[:, 6 * k:6 * k + 6]
+
+    send_two([(nxt, T.lprev[:], wcols(nxt), "l_prev"), (prv, T.lnext[:], wcols(prv), "l_next")])
+    send(opp, T.lopp[:], wcols(opp), "l_opp")
+
+    wait("V", e_slot)
+    v1 = done(V.tensor_scalar(T.u1[:], T.sl[:], 4, None, AluOpType.arith_shift_right))
+    v2 = done(V.tensor_scalar(T.u2[:], T.sl[:], 24, None, mult))
+    v_p16 = done(V.tensor_copy(T.pos16[:], T.sl[:]))
+    wait("V", v1)
+    v3 = done(V.tensor_scalar(T.u3[:], T.u1[:], 1 - SLOTS, None, mult))
+    wait("g", v_p16)
+    send_two([(nxt, T.pprev[:], T.pos16[:], "p_prev"), (prv, T.pnext[:], T.pos16[:], "p_next")])
+    wait("V", v2, v3)
+    v_s = [done(V.tensor_tensor(T.so[:, 16 * j:16 * j + 16], T.u2[:], T.u3[:], add)) for j in range(2)]
+    wait("V", *v_s)
+    v_t = done(V.transpose(T.sot[:], T.so[:]))
+    wait("V", v_t)
+    v_o = done(V.tensor_copy(T.so16[:], T.sot[:, 0:16]))
+    wait("V", e_own, a_flat, v_o)
+    v_sc = done(V.tensor_copy(T.flat[:].indirect(T.so16[:]), T.ol[:]))
+    wait("SY", v_sc)
+    for k in range(8):
+        load(SY, T.ownf[16 * k:16 * k + 16, :], T.flat[0:1, :], e_of)
+
+    def xwin(t):
+        return T.xs[:, t:4 * R]
+
+    def gather(tile, off):
+        ev = []
+        for t in range(4):
+            out, src = tile[:, t:4 * CAPP:4], xwin(t).indirect(off)
+            ev.append(done(V.tensor_copy(out, src)) if t < 2 else done(A.activation(out, src, COPY)))
+        return ev
+
+    wait("V", *a_e)
+    v_qe = done(V.quantize_mx(T.ec[:], T.ep[:], T.et[:]))
+    for q in ("V", "A"):
+        wait(q, e_x, v_w16)
+    ev = gather(T.tself, wcols(r))
+    wait("V", v_pad["self"], *ev)
+    v_qs = done(V.quantize_mx(T.lc[:, L_SELF:L_SELF + 128], T.lp[:, L_SELF:L_SELF + 128], T.tself[:]))
+    for k, name, back, at, n in ((nxt, "next", "f_prev", L_PREV, nh), (prv, "prev", "f_next", L_NEXT, nh),
+                                 (opp, "opp", "f_opp", L_OPP, ne)):
+        for q in ("V", "A"):
+            wait(q, ("l_" + name, n))
+        ev = gather(T["t" + name], T["l" + name][:])
+        wait("V", v_pad[name], *ev)
+        e = done(V.quantize_mx(T["c" + name][:], T["s" + name][:], T["t" + name][:]))
+        wait("g", e)
+        send(k, u8(T.lc[:, at:at + CAPP]), u8(T["c" + name][:, 0:CAPP]), back)
+        send(k, T.lp[:, at:at + CAPP], T["s" + name][:, 0:CAPP], back)
+
+    wait("V", e_of)
+    v_own = done(V.tensor_scalar(T.own16[:], T.ownf[:], 4, None, mult))
+    for q in ("V", "A"):
+        wait(q, v_own)
+
+    def own_columns(h, t, q):
+        out, src = T["xh%d" % h][:, 2 * CAPP * t:2 * CAPP * t + 2 * CAPP], xwin(t).indirect(T.own16[:, 12 * h:12 * h + 12])
+        return done(V.tensor_scalar(out, src, 0.5, None, mult) if q == "V" else A.activation(out, src, COPY, scale=0.5))
+
+    ev_x = {r // 2: [own_columns(r // 2, t, "VVAA"[t]) for t in range(4)],
+            1 - r // 2: [own_columns(1 - r // 2, t, "A") for t in range(3)]}
+
+    v_m, v_q = {}, {}
+    for i, (q, at, skip, arr) in enumerate(((r, L_SELF, 0, v_qs), (prv, L_PREV, 0, ("f_prev", 2 * ne)),
+                                            (nxt, L_NEXT - PAD, PAD, ("f_next", 2 * ne)),
+                                            (opp, L_OPP, 0, ("f_opp", 2 * ne)))):
+        bank, h, c = 4 * (i % 2), q // 2, CAPP * (q % 2)
+        m0 = CAPP * i
+        wait("PE", v_qe, arr)
+        dec, v_m[i] = [], []
+        for b in range(4):
+            if i > 1:
+                wait("PE", v_m[i - 2][b])
+            dec.append(done(PE.matmul_mx(T["ps%d" % (bank + b)][:, 0:128], T.ec[:, 128 * b:128 * b + 128], T.ep[:, 128 * b:128 * b + 128],
+                                         T.lc[:, at:at + 128], T.lp[:, at:at + 128], True, True)))
+        for b in range(4):
+            wait("V", dec[b], ev_x[h][b])
+            v_m[i].append(done(V.tensor_tensor(T["mt%d" % i][:, b:4 * CAPP:4], T["ps%d" % (bank + b)][:, skip:skip + CAPP],
+                                               T["xh%d" % h][:, 2 * CAPP * b + c:2 * CAPP * b + c + CAPP], add)))
+        wait("V", v_mpad[i], *v_m[i])
+        if i:
+            wait("V", v_q[i - 1])
+        v_q[i] = done(V.quantize_mx(T.mc[:, m0:m0 + 128], T.mp[:, m0:m0 + 128], T["mt%d" % i][:]))
+        wait("g", v_q[i])
+        two = [(k, u8(land[:, m0:m0 + CAPP]), u8(T.mc[:, m0:m0 + CAPP]), "m_%s%d" % (name, i))
+               for k, land, name in ((nxt, T.prevc, "prev"), (prv, T.nextc, "next"))]
+        if i < 3:
+            send_two(two)
+        else:
+            send_two([(nxt, T.prevp[:], T.mp[:, 0:SLOTS], "m_prevp"), (prv, T.nextp[:], T.mp[:, 0:SLOTS], "m_nextp")])
+            for w in two:
+                send(*w)
+        if i == 0:
+            ev_x[1 - r // 2].append(own_columns(1 - r // 2, 3, "V"))
+    wait("V", e_w)
+    v_qw = done(V.quantize_mx(T.wc[:], T.wp[:], T.ws[:]))
+
+    def product(bank, codes, plane, a, n):
+        return done(PE.matmul_mx(T["ps%d" % bank][:, 0:n], T.wc[:], T.wp[:], codes[:, a:a + n], plane[:, a:a + n], True, True))
+
+    def copy(q, out, src):
+        return done(V.tensor_copy(out, src) if q == "V" else A.activation(out, src, COPY))
+
+    def unload(q, win, s, bank, first, blocks):
+        order = (s, (s - 1) % N, (s + 1) % N, (s + 2) % N)
+        return [copy(q, win[:, CAPP * order[j]:CAPP * order[j] + CAPP], T["ps%d" % bank][:, CAPP * j - first:CAPP * j - first + CAPP])
+                for j in blocks]
+
+    def gather_out(q, out, win, off, j, n):
+        return copy(q, out[:, j:j + n], win[:].indirect(off[:, j // 16:(j + n) // 16]))
+
+    wait("PE", v_qw, *[e for i in v_m for e in v_m[i]], *[v_q[i] for i in v_q])
+    p = product(0, T.mc, T.mp, 0, SLOTS)
+    wait("A", p)
+    a_own = unload("A", T.yw1, r, 0, 0, range(4))
+    wait("A", v_p16, *a_own)
+    a_y1 = gather_out("A", T.ys1, T.yw1, T.pos16, 0, S)
+    wait("SY", a_y1)
+    load(SY, T.y[:, S:2 * S], T.ys1[:], e_y)
+    sides = (("prev", prv, T.prevc, T.prevp, T.yw0), ("next", nxt, T.nextc, T.nextp, T.yw2))
+    copies = {}
+    for j, (name, s, c, pl, win) in enumerate(sides):
+        wait("PE", *[("m_%s%s" % (name, e), nh) for e in "012p"])
+        p = product(1 + j, c, pl, 0, 3 * CAPP)
+        wait("VA"[j], p)
+        copies[name] = unload("VA"[j], win, s, 1 + j, 0, range(3))
+    for j, (name, s, c, pl, win) in enumerate(sides):
+        wait("PE", ("m_%s3" % name, ne))
+        p = product(3 + j, c, pl, SLOTS - 128, 128)
+        wait("V", p)
+        copies[name] += unload("V", win, s, 3 + j, SLOTS - 128, (3,))
+        out, off, at = (T.ys0, T.pprev, 0) if j == 0 else (T.ys2, T.pnext, 2 * S)
+        for q, a, sq in (("V", 0, "SY"), ("A", 128, "A" if j else "SY")):
+            wait(q, ("p_" + name, nh), *copies[name])
+            e = gather_out(q, out, win, off, a, 128)
+            wait(sq, e)
+            load(queues[sq], T.y[:, at + a:at + a + 128], out[:, a:a + 128], e_y)
+
+    wait("g", e_y, ("sent", sent[0]))
+    wait("g", *list(unwaited.items()))

@@ -5,55 +5,121 @@ N, S, CAPP, R = 4, 256, 96, 1024
 SLOTS = N * CAPP
 PAD = 128 - CAPP
 F8 = "float8_e4m3fn_x4"
-L_OPP, L_PREV, L_SELF, L_NEXT, L_ALL = 0, CAPP, 2 * CAPP, 3 * CAPP + PAD, 4 * CAPP + PAD
+L_AT = {"o": 0, "a": CAPP, "s": 2 * CAPP, "b": 3 * CAPP + PAD}
+L_ALL = 4 * CAPP + PAD
 M_ALL = SLOTS + PAD
+ROUTE = ({"a": 0, "b": 0}, {"a": None, "b": 1}, {"a": None, "b": 1}, {"a": None, "b": None})
 
 SCRATCH = {
     "xs": ("sbuf", [128, 4 * R], "bfloat16"),
     "ws": ("sbuf", [128, 512], "bfloat16"),
     "wl": ("sbuf", [128, 24], "int32"), "sl": ("sbuf", [128, 16], "int32"), "ol": ("sbuf", [128, 256], "int32"),
     "w16": ("sbuf", [128, 24], "uint16"),
-    "lopp": ("sbuf", [128, 6], "uint16"), "lnext": ("sbuf", [128, 6], "uint16"), "lprev": ("sbuf", [128, 6], "uint16"),
     "u1": ("sbuf", [128, 16], "int32"), "u2": ("sbuf", [128, 16], "int32"), "u3": ("sbuf", [128, 16], "int32"),
-    "pos16": ("sbuf", [128, 16], "uint16"), "pprev": ("sbuf", [128, 16], "uint16"), "pnext": ("sbuf", [128, 16], "uint16"),
+    "pos16": ("sbuf", [128, 16], "uint16"), "hpos": ("sbuf", [128, 16], "uint16"),
     "so": ("sbuf", [128, 32], "float32"), "sot": ("sbuf", [128, 32], "float32"), "so16": ("sbuf", [128, 16], "uint16"),
     "flat": ("sbuf", [128, SLOTS], "float32"), "ownf": ("sbuf", [128, 24], "float32"), "own16": ("sbuf", [128, 24], "uint16"),
-    "half": ("sbuf", [128, 512], "bfloat16"), "ident": ("sbuf", [128, 128], "bfloat16"),
-    "et": ("sbuf", [128, 2048], "bfloat16"), "ec": ("sbuf", [128, 512], F8), "ep": ("sbuf", [128, 512], "uint8"),
+    "half": ("sbuf", [128, 128], "bfloat16"), "ident": ("sbuf", [128, 128], "bfloat16"),
+    "et": ("sbuf", [128, 516], "bfloat16"), "ec": ("sbuf", [128, 512], F8), "ep": ("sbuf", [128, 512], "uint8"),
     "wc": ("sbuf", [128, 128], F8), "wp": ("sbuf", [128, 128], "uint8"),
-    "tself": ("sbuf", [128, 512], "bfloat16"),
+    "ts": ("sbuf", [128, 512], "bfloat16"),
     "lc": ("sbuf", [128, L_ALL], F8), "lp": ("sbuf", [128, L_ALL], "uint8"),
     "mc": ("sbuf", [128, M_ALL], F8), "mp": ("sbuf", [128, M_ALL], "uint8"),
-    "prevc": ("sbuf", [128, SLOTS], F8), "prevp": ("sbuf", [128, SLOTS], "uint8"),
-    "nextc": ("sbuf", [128, SLOTS], F8), "nextp": ("sbuf", [128, SLOTS], "uint8"),
+    "hc": ("sbuf", [128, SLOTS], F8), "hp": ("sbuf", [128, SLOTS], "uint8"),
 }
-for _k in ("next", "prev", "opp"):
+for _k in "abo":
+    SCRATCH["ask_" + _k] = ("sbuf", [128, 6], "uint16")
     SCRATCH["t" + _k] = ("sbuf", [128, 512], "bfloat16")
     SCRATCH["c" + _k] = ("sbuf", [128, 128], F8)
-    SCRATCH["s" + _k] = ("sbuf", [128, 128], "uint8")
+    SCRATCH["p" + _k] = ("sbuf", [128, 128], "uint8")
+for _k in "ab":
+    SCRATCH["mc_" + _k] = ("sbuf", [128, SLOTS], F8)
+    SCRATCH["mp_" + _k] = ("sbuf", [128, SLOTS], "uint8")
+    SCRATCH["pos_" + _k] = ("sbuf", [128, 16], "uint16")
 for _k in range(2):
     SCRATCH["xh%d" % _k] = ("sbuf", [128, 8 * CAPP], "bfloat16")
 for _k in range(4):
     SCRATCH["mt%d" % _k] = ("sbuf", [128, 512], "bfloat16")
-for _k in range(3):
-    SCRATCH["yw%d" % _k] = ("sbuf", [128, SLOTS], "float32")
-    SCRATCH["ys%d" % _k] = ("sbuf", [128, S], "float32")
+for _k in "sab":
+    SCRATCH["yw" + _k] = ("sbuf", [128, SLOTS], "float32")
+    SCRATCH["ys" + _k] = ("sbuf", [128, S], "float32")
 for _k in range(8):
     SCRATCH["ps%d" % _k] = ("psum", [128, 512], "float32")
-ARR = ["sent", "l_opp", "l_next", "l_prev", "p_next", "p_prev", "f_opp", "f_next", "f_prev",
-       "m_next0", "m_next1", "m_next2", "m_next3", "m_nextp", "m_prev0", "m_prev1", "m_prev2", "m_prev3", "m_prevp"]
-SEMAPHORES = ARR + ["e%d" % _k for _k in range(130)]
+ARR = (["sent", "h_pos", "h0", "h1", "h2", "p_a", "p_b"] + [_s + _k for _s in ("l_", "f_") for _k in "abo"]
+       + ["m_%s%d" % (_k, _i) for _k in "ab" for _i in range(4)])
+SEMAPHORES = ARR + ["e%d" % _k for _k in range(125)]
+
+
+def peers(r):
+    a = r ^ 1
+    return {"s": r, "a": a, "b": (2 * r - a) % N, "o": (r + 2) % N}
+
+
+def helpers(T, topo, r):
+    home, p = T.cores[r], peers(r)
+    return [c for c in topo.cores_of(home) if topo.die(c) != topo.die(home)
+            and all(topo.may_write(c, T.cores[p[k]]) for k in "ab")][:2]
+
+
+def u8(v):
+    return v.bitcast(dt.uint8)
+
+
+def block(codes, plane, i):
+    return u8(codes[:, CAPP * i:CAPP * i + CAPP]), plane[:, CAPP * i:CAPP * i + CAPP]
+
+
+def writer(g, core, T, topo):
+    sent = [0]
+
+    def send(*items):
+        tr = []
+        for to, out, src, sem, es in items:
+            rid, pid, _ = topo.addr(to)
+            sent[0] += len(es)
+            mask = sum(1 << e for e in es)
+            if len(items) == 1:
+                g.remote_dma(out_ap=out, in_ap=src, remote_sem=T.sem[sem], local_sem=T.sem.sent, pid=pid, routing_id=rid,
+                             dma_engine_mask=mask)
+                return
+            tr.append(RemoteDMATransfer(dst_ids=[DstId(rid=rid, pnc=pid)], dma_engine_mask=mask,
+                                        remote_sem=T.sem[sem], srcs=[src], dsts=[out]))
+        g.remote_dma_fused(tr, local_sem=T.sem.sent)
+    return send, sent
+
+
+def helper_program(g, core, T, topo, r, h):
+    send, sent = writer(g, core, T, topo)
+    home, p = T.cores[r], peers(r)
+    out = topo.engines(core, T.cores[p["a"]])
+    near = [e for e in topo.engines(home, core) if e not in topo.engines(home, T.cores[p["a"]])]
+    k = "ab"[h]
+    g.wait_ge(T.sem.h_pos, len(near) // 2)
+    send((T.cores[p[k]], T["pos_" + k][:], T.hpos[:], "p_" + k, out))
+    for i, route in enumerate(ROUTE):
+        sides = [k for k in "ab" if route[k] == h]
+        if sides:
+            g.wait_ge(T.sem["h%d" % i], 2 * len(near))
+        for k in sides:
+            for land, src in zip(block(T["mc_" + k], T["mp_" + k], i), block(T.hc, T.hp, i)):
+                send((T.cores[p[k]], land, src, "m_%s%d" % (k, i), out))
+    g.wait_ge(T.sem.sent, sent[0])
 
 
 def rank_program(g, core, T, topo):
     r = T.rank_of(core)
     if r is None:
+        for q in range(N):
+            if core in helpers(T, topo, q):
+                helper_program(g, core, T, topo, q, helpers(T, topo, q).index(core))
         return
     V, A, PE, SY = g.vector, g.scalar, g.tensor, g.sync
     queues = {"g": g, "V": V, "A": A, "PE": PE, "SY": SY}
     add, mult = AluOpType.add, AluOpType.mult
     COPY = ActivationFunctionType.Copy
-    nxt, prv, opp = (r + 1) % N, (r - 1) % N, (r + 2) % N
+    peer = peers(r)
+    to = {k: T.cores[peer[k]] for k in "abo"}
+    hands = helpers(T, topo, r)
     nevents = [0]
     seen = set()
     unwaited = {}
@@ -71,131 +137,117 @@ def rank_program(g, core, T, topo):
                 unwaited.pop(name, None)
                 queues[q].wait_ge(T.sem[name], n)
 
-    def done(ins, n=1):
-        e = event(n)
-        ins.then_inc(T.sem[e[0]], n)
+    def done(*calls):
+        e = event(len(calls))
+        for ins in calls:
+            ins.then_inc(T.sem[e[0]], 1)
         return e
 
-    sent = [0]
-
-    def engs(k):
-        return topo.engines(core, T.cores[k])
-
-    def send(k, out, src, sem):
-        rid, pid, _ = topo.addr(T.cores[k])
-        g.remote_dma(out_ap=out, in_ap=src, remote_sem=T.sem[sem], local_sem=T.sem.sent, pid=pid, routing_id=rid,
-                     dma_engine_mask=topo.mask(core, T.cores[k]))
-        sent[0] += len(engs(k))
-
-    def send_two(items):
-        tr = []
-        for i, (k, out, src, sem) in enumerate(items):
-            es = engs(k)
-            es = es[i * len(es) // 2:(i + 1) * len(es) // 2]
-            sent[0] += len(es)
-            rid, pid, _ = topo.addr(T.cores[k])
-            tr.append(RemoteDMATransfer(dst_ids=[DstId(rid=rid, pnc=pid)], dma_engine_mask=sum(1 << e for e in es),
-                                        remote_sem=T.sem[sem], srcs=[src], dsts=[out]))
-        g.remote_dma_fused(tr, local_sem=T.sem.sent)
-
-    ne = len(engs(opp))
+    send, sent = writer(g, core, T, topo)
+    far = topo.engines(core, to["a"])
+    near = [e for e in topo.engines(core, hands[0]) if e not in far]
+    ne = len(far)
     nh = ne // 2
+    halves = {"a": far[:nh], "b": far[nh:]}
 
-    def u8(v):
-        return v.bitcast(dt.uint8)
-
-    e_want, e_slot, e_own, e_x, e_w, e_of, e_y = (event(128), event(128), event(16), event(16), event(16), event(128), event(80))
+    e_want, e_slot, e_own, e_x, e_w, e_of, e_y = (event(32), event(32), event(16), event(16), event(16), event(64), event(96))
 
     def load(q, out, src, e):
         q.dma_start(out, src).then_inc(T.sem[e[0]], 16)
 
-    for k in range(4):
-        load(SY, T.wl[16 * k:16 * k + 16, :], T.want[:], e_want)
-        load(A, T.wl[16 * k + 64:16 * k + 80, :], T.want[:], e_want)
-    for k in range(4):
-        load(SY, T.sl[16 * k:16 * k + 16, :], T.slot[:], e_slot)
-        load(A, T.sl[16 * k + 64:16 * k + 80, :], T.slot[:], e_slot)
+    v_half = done(V.memset(T.half[:], 0.5))
+    v_ol = done(V.memset(T.ol[:], 0))
+    for k, q in enumerate((SY, A)):
+        load(q, T.wl[16 * k:16 * k + 16, :], T.want[:], e_want)
+        load(q, T.sl[16 * k:16 * k + 16, :], T.slot[:], e_slot)
+    wait("SY", v_ol)
+    load(SY, T.ol[0:1, :], T.own[:], e_own)
     load(SY, T.xs[:], T.x[:], e_x)
 
-    v_ol = done(V.memset(T.ol[:], 0))
-    v_half = done(V.memset(T.half[:], 0.5))
-    v_pad = {k: done(V.memset(T["t" + k][:, 4 * CAPP:512], 0.0)) for k in ("next", "prev", "opp", "self")}
-    v_mpad = [done(V.memset(T["mt%d" % i][:, 4 * CAPP:512], 0.0)) for i in range(4)]
-    z = [done(V.memset(T.et[:, 512 * b:512 * b + 512], 0.0)) for b in (0, 1)]
-    wait("A", v_ol)
-    load(A, T.ol[0:1, :], T.own[:], e_own)
-    load(A, T.ws[:], T.w[:], e_w)
+    g_so = done(g.iota(T.so[:], [[0, 2], [16, 16]], 0, 1, allow_small_or_imprecise_dtypes=True))
     wait("g", v_half)
-    g_id = done(g.affine_select(T.ident[:], T.half[:, 0:128], [[-1, 128]], AluOpType.is_equal, 0.0, 0, 1))
+    g_id = done(g.affine_select(T.ident[:], T.half[:], [[-1, 128]], AluOpType.is_equal, 0.0, 0, 1))
+    v_z = done(V.memset(T.et[:], 0.0))
+    wait("V", g_id, v_z)
+    v_e = done(V.tensor_copy(T.et[:, 3:512:4], T.ident[:]))
+    wait("V", v_e)
+    v_qe = done(*[V.quantize_mx(T.ec[:, 128 * b:128 * b + 128], T.ep[:, 128 * b:128 * b + 128], T.et[:, 3 - b:515 - b])
+                  for b in range(4)])
     wait("A", v_half)
-    a_flat = done(A.activation(T.flat[:], T.half[:, 0:SLOTS], COPY, scale=0.0))
-    z += [done(A.activation(T.et[:, 512 * b:512 * b + 512], T.half[:], COPY, scale=0.0)) for b in (2, 3)]
-    wait("A", g_id)
-    a_e = []
-    for b in range(4):
-        wait("A", z[b])
-        a_e.append(done(A.activation(T.et[:, 512 * b + b:512 * b + 512:4], T.ident[:], COPY)))
+    a_flat = done(*[A.activation(T.flat[:, 128 * j:128 * j + 128], T.half[:], COPY, scale=0.0) for j in range(3)])
+    a_pad = done(*[A.activation(T[k][:, 4 * CAPP:512], T.half[:], COPY, scale=0.0)
+                   for k in ("ta", "tb", "to", "ts", "mt0", "mt1", "mt2", "mt3")])
 
     wait("V", e_want)
-    v_w16 = done(V.tensor_scalar(T.w16[:], T.wl[:], 0, 4, AluOpType.max, mult))
+    v_w16 = done(*[V.tensor_scalar(T.w16[p:p + 32, :], T.wl[0:32, :], 0, 4, AluOpType.max, mult) for p in range(0, 128, 32)])
     wait("g", v_w16)
 
     def wcols(k):
-        return T.w16[:, 6 * k:6 * k + 6]
+        return T.w16[:, 6 * peer[k]:6 * peer[k] + 6]
 
-    send_two([(nxt, T.lprev[:], wcols(nxt), "l_prev"), (prv, T.lnext[:], wcols(prv), "l_next")])
-    send(opp, T.lopp[:], wcols(opp), "l_opp")
+    send(*[(to[k], T["ask_" + k][:], wcols(k), "l_" + k, halves[k]) for k in "ab"])
+    send((to["o"], T.ask_o[:], wcols("o"), "l_o", far))
+
+    v_p16 = event(4)
+
+    def positions(p):
+        V.tensor_copy(T.pos16[p:p + 32, :], T.sl[0:32, :]).then_inc(T.sem[v_p16[0]], 1)
 
     wait("V", e_slot)
-    v1 = done(V.tensor_scalar(T.u1[:], T.sl[:], 4, None, AluOpType.arith_shift_right))
-    v2 = done(V.tensor_scalar(T.u2[:], T.sl[:], 24, None, mult))
-    v_p16 = done(V.tensor_copy(T.pos16[:], T.sl[:]))
+    v1 = done(V.tensor_scalar(T.u1[0:16, :], T.sl[0:16, :], 4, None, AluOpType.arith_shift_right))
+    v2 = done(V.tensor_scalar(T.u2[0:16, :], T.sl[0:16, :], 24, None, mult))
     wait("V", v1)
-    v3 = done(V.tensor_scalar(T.u3[:], T.u1[:], 1 - SLOTS, None, mult))
-    wait("g", v_p16)
-    send_two([(nxt, T.pprev[:], T.pos16[:], "p_prev"), (prv, T.pnext[:], T.pos16[:], "p_next")])
-    wait("V", v2, v3)
-    v_s = [done(V.tensor_tensor(T.so[:, 16 * j:16 * j + 16], T.u2[:], T.u3[:], add)) for j in range(2)]
-    wait("V", *v_s)
+    v3 = done(V.tensor_scalar(T.u3[0:16, :], T.u1[0:16, :], 1 - SLOTS, None, mult))
+    positions(0)
+    wait("V", v2, v3, g_so)
+    v_s = done(V.tensor_tensor(T.so[0:16, 0:16], T.u2[0:16, :], T.u3[0:16, :], add))
+    positions(32)
+    wait("V", v_s)
     v_t = done(V.transpose(T.sot[:], T.so[:]))
+    positions(64)
     wait("V", v_t)
     v_o = done(V.tensor_copy(T.so16[:], T.sot[:, 0:16]))
-    wait("V", e_own, a_flat, v_o)
+    positions(96)
+    wait("g", v_p16)
+    send(*[(hands[h], T.hpos[:], T.pos16[:], "h_pos", near[h * len(near) // 2:(h + 1) * len(near) // 2]) for h in range(2)])
+    wait("V", e_own, v_o, a_flat)
     v_sc = done(V.tensor_copy(T.flat[:].indirect(T.so16[:]), T.ol[:]))
     wait("SY", v_sc)
-    for k in range(8):
+    for k in range(4):
         load(SY, T.ownf[16 * k:16 * k + 16, :], T.flat[0:1, :], e_of)
+    load(SY, T.ws[:], T.w[:], e_w)
 
     def xwin(t):
         return T.xs[:, t:4 * R]
 
     def gather(tile, off):
-        ev = []
+        calls = []
         for t in range(4):
             out, src = tile[:, t:4 * CAPP:4], xwin(t).indirect(off)
-            ev.append(done(V.tensor_copy(out, src)) if t < 2 else done(A.activation(out, src, COPY)))
-        return ev
+            calls.append(V.tensor_copy(out, src) if t < 2 else A.activation(out, src, COPY))
+        return done(*calls)
 
-    wait("V", *a_e)
-    v_qe = done(V.quantize_mx(T.ec[:], T.ep[:], T.et[:]))
     for q in ("V", "A"):
-        wait(q, e_x, v_w16)
-    ev = gather(T.tself, wcols(r))
-    wait("V", v_pad["self"], *ev)
-    v_qs = done(V.quantize_mx(T.lc[:, L_SELF:L_SELF + 128], T.lp[:, L_SELF:L_SELF + 128], T.tself[:]))
-    for k, name, back, at, n in ((nxt, "next", "f_prev", L_PREV, nh), (prv, "prev", "f_next", L_NEXT, nh),
-                                 (opp, "opp", "f_opp", L_OPP, ne)):
+        wait(q, e_x)
+    for k, n in (("a", nh), ("b", nh), ("o", ne)):
         for q in ("V", "A"):
-            wait(q, ("l_" + name, n))
-        ev = gather(T["t" + name], T["l" + name][:])
-        wait("V", v_pad[name], *ev)
-        e = done(V.quantize_mx(T["c" + name][:], T["s" + name][:], T["t" + name][:]))
+            wait(q, ("l_" + k, n))
+        e = gather(T["t" + k], T["ask_" + k][:])
+        wait("V", a_pad, e)
+        e = done(V.quantize_mx(T["c" + k][:], T["p" + k][:], T["t" + k][:]))
         wait("g", e)
-        send(k, u8(T.lc[:, at:at + CAPP]), u8(T["c" + name][:, 0:CAPP]), back)
-        send(k, T.lp[:, at:at + CAPP], T["s" + name][:, 0:CAPP], back)
-
+        at = L_AT[k]
+        send((to[k], u8(T.lc[:, at:at + CAPP]), u8(T["c" + k][:, 0:CAPP]), "f_" + k, far))
+        send((to[k], T.lp[:, at:at + CAPP], T["p" + k][:, 0:CAPP], "f_" + k, far))
+    for q in ("V", "A"):
+        wait(q, v_w16)
+    e = gather(T.ts, wcols("s"))
     wait("V", e_of)
-    v_own = done(V.tensor_scalar(T.own16[:], T.ownf[:], 4, None, mult))
+    v_own = done(*[V.tensor_scalar(T.own16[p:p + 64, :], T.ownf[0:64, :], 4, None, mult) for p in (0, 64)])
+    wait("V", e)
+    at = L_AT["s"]
+    v_qs = done(V.quantize_mx(T.lc[:, at:at + 128], T.lp[:, at:at + 128], T.ts[:]))
+
     for q in ("V", "A"):
         wait(q, v_own)
 
@@ -204,83 +256,74 @@ def rank_program(g, core, T, topo):
         return done(V.tensor_scalar(out, src, 0.5, None, mult) if q == "V" else A.activation(out, src, COPY, scale=0.5))
 
     ev_x = {r // 2: [own_columns(r // 2, t, "VVAA"[t]) for t in range(4)],
-            1 - r // 2: [own_columns(1 - r // 2, t, "A") for t in range(3)]}
+            1 - r // 2: [own_columns(1 - r // 2, t, "A") for t in range(4)]}
 
     v_m, v_q = {}, {}
-    for i, (q, at, skip, arr) in enumerate(((r, L_SELF, 0, v_qs), (prv, L_PREV, 0, ("f_prev", 2 * ne)),
-                                            (nxt, L_NEXT - PAD, PAD, ("f_next", 2 * ne)),
-                                            (opp, L_OPP, 0, ("f_opp", 2 * ne)))):
+    for i, k in enumerate("sabo"):
+        q = peer[k]
+        skip = PAD if k == "b" else 0
+        at = L_AT[k] - skip
         bank, h, c = 4 * (i % 2), q // 2, CAPP * (q % 2)
         m0 = CAPP * i
-        wait("PE", v_qe, arr)
+        wait("PE", v_qe, ("f_" + k, 2 * ne) if i else v_qs)
         dec, v_m[i] = [], []
         for b in range(4):
             if i > 1:
-                wait("PE", v_m[i - 2][b])
+                wait("PE", v_q[i - 2])
             dec.append(done(PE.matmul_mx(T["ps%d" % (bank + b)][:, 0:128], T.ec[:, 128 * b:128 * b + 128], T.ep[:, 128 * b:128 * b + 128],
                                          T.lc[:, at:at + 128], T.lp[:, at:at + 128], True, True)))
         for b in range(4):
             wait("V", dec[b], ev_x[h][b])
-            v_m[i].append(done(V.tensor_tensor(T["mt%d" % i][:, b:4 * CAPP:4], T["ps%d" % (bank + b)][:, skip:skip + CAPP],
-                                               T["xh%d" % h][:, 2 * CAPP * b + c:2 * CAPP * b + c + CAPP], add)))
-        wait("V", v_mpad[i], *v_m[i])
+            v_m[i].append(V.tensor_tensor(T["mt%d" % i][:, b:4 * CAPP:4], T["ps%d" % (bank + b)][:, skip:skip + CAPP],
+                                          T["xh%d" % h][:, 2 * CAPP * b + c:2 * CAPP * b + c + CAPP], add))
+        wait("V", done(*v_m[i]))
         if i:
             wait("V", v_q[i - 1])
         v_q[i] = done(V.quantize_mx(T.mc[:, m0:m0 + 128], T.mp[:, m0:m0 + 128], T["mt%d" % i][:]))
         wait("g", v_q[i])
-        two = [(k, u8(land[:, m0:m0 + CAPP]), u8(T.mc[:, m0:m0 + CAPP]), "m_%s%d" % (name, i))
-               for k, land, name in ((nxt, T.prevc, "prev"), (prv, T.nextc, "next"))]
-        if i < 3:
-            send_two(two)
+        straight = [k for k in "ab" if ROUTE[i][k] is None]
+        via = sorted(set(ROUTE[i].values()) - {None})
+        src = block(T.mc, T.mp, i)
+        land = {k: block(T["mc_" + k], T["mp_" + k], i) for k in "ab"}
+        if via:
+            for j in range(2):
+                send(*[(to[k], land[k][j], src[j], "m_%s%d" % (k, i), far) for k in straight],
+                     (hands[via[0]], block(T.hc, T.hp, i)[j], src[j], "h%d" % i, near))
         else:
-            send_two([(nxt, T.prevp[:], T.mp[:, 0:SLOTS], "m_prevp"), (prv, T.nextp[:], T.mp[:, 0:SLOTS], "m_nextp")])
-            for w in two:
-                send(*w)
-        if i == 0:
-            ev_x[1 - r // 2].append(own_columns(1 - r // 2, 3, "V"))
+            send(*[(to[k], land[k][1], src[1], "m_%s%d" % (k, i), halves[k]) for k in "ab"])
+            for k in "ab":
+                send((to[k], land[k][0], src[0], "m_%s%d" % (k, i), far))
     wait("V", e_w)
     v_qw = done(V.quantize_mx(T.wc[:], T.wp[:], T.ws[:]))
 
-    def product(bank, codes, plane, a, n):
-        return done(PE.matmul_mx(T["ps%d" % bank][:, 0:n], T.wc[:], T.wp[:], codes[:, a:a + n], plane[:, a:a + n], True, True))
-
     def copy(q, out, src):
-        return done(V.tensor_copy(out, src) if q == "V" else A.activation(out, src, COPY))
+        return V.tensor_copy(out, src) if q == "V" else A.activation(out, src, COPY)
 
-    def unload(q, win, s, bank, first, blocks):
-        order = (s, (s - 1) % N, (s + 1) % N, (s + 2) % N)
-        return [copy(q, win[:, CAPP * order[j]:CAPP * order[j] + CAPP], T["ps%d" % bank][:, CAPP * j - first:CAPP * j - first + CAPP])
-                for j in blocks]
+    def product(q, bank, k, blocks):
+        codes, plane = (T.mc, T.mp) if k == "s" else (T["mc_" + k], T["mp_" + k])
+        if k != "s":
+            wait("PE", *[("m_%s%d" % (k, j), 2 * ne if j < 3 else ne + nh) for j in blocks])
+        end = CAPP * blocks[-1] + CAPP
+        first = min(CAPP * blocks[0], end - 128)
+        ps = T["ps%d" % bank]
+        wait(q, done(PE.matmul_mx(ps[:, 0:end - first], T.wc[:], T.wp[:], codes[:, first:end], plane[:, first:end], True, True)))
+        order = [peers(peer[k])[j] for j in "sabo"]
+        return done(*[copy(q, T["yw" + k][:, CAPP * order[j]:CAPP * order[j] + CAPP], ps[:, CAPP * j - first:CAPP * j - first + CAPP])
+                      for j in blocks])
 
-    def gather_out(q, out, win, off, j, n):
-        return copy(q, out[:, j:j + n], win[:].indirect(off[:, j // 16:(j + n) // 16]))
-
-    wait("PE", v_qw, *[e for i in v_m for e in v_m[i]], *[v_q[i] for i in v_q])
-    p = product(0, T.mc, T.mp, 0, SLOTS)
-    wait("A", p)
-    a_own = unload("A", T.yw1, r, 0, 0, range(4))
-    wait("A", v_p16, *a_own)
-    a_y1 = gather_out("A", T.ys1, T.yw1, T.pos16, 0, S)
-    wait("SY", a_y1)
-    load(SY, T.y[:, S:2 * S], T.ys1[:], e_y)
-    sides = (("prev", prv, T.prevc, T.prevp, T.yw0), ("next", nxt, T.nextc, T.nextp, T.yw2))
-    copies = {}
-    for j, (name, s, c, pl, win) in enumerate(sides):
-        wait("PE", *[("m_%s%s" % (name, e), nh) for e in "012p"])
-        p = product(1 + j, c, pl, 0, 3 * CAPP)
-        wait("VA"[j], p)
-        copies[name] = unload("VA"[j], win, s, 1 + j, 0, range(3))
-    for j, (name, s, c, pl, win) in enumerate(sides):
-        wait("PE", ("m_%s3" % name, ne))
-        p = product(3 + j, c, pl, SLOTS - 128, 128)
-        wait("V", p)
-        copies[name] += unload("V", win, s, 3 + j, SLOTS - 128, (3,))
-        out, off, at = (T.ys0, T.pprev, 0) if j == 0 else (T.ys2, T.pnext, 2 * S)
-        for q, a, sq in (("V", 0, "SY"), ("A", 128, "A" if j else "SY")):
-            wait(q, ("p_" + name, nh), *copies[name])
-            e = gather_out(q, out, win, off, a, 128)
+    def finish(k, off, ready, stores):
+        at = S * ((peer[k] - r + 1) % N)
+        for q, a, sq in (("V", 0, stores[0]), ("A", 128, stores[1])):
+            wait(q, *ready)
+            e = done(copy(q, T["ys" + k][:, a:a + 128], T["yw" + k][:].indirect(off[:, a // 16:a // 16 + 8])))
             wait(sq, e)
-            load(queues[sq], T.y[:, at + a:at + a + 128], out[:, a:a + 128], e_y)
+            load(queues[sq], T.y[:, at + a:at + a + 128], T["ys" + k][:, a:a + 128], e_y)
 
-    wait("g", e_y, ("sent", sent[0]))
-    wait("g", *list(unwaited.items()))
+    wait("PE", v_qw, *v_q.values())
+    finish("s", T.pos16, [product("A", 0, "s", (0, 1)), product("V", 1, "s", (2, 3)), v_p16], ("SY", "SY"))
+    finish("a", T.pos_a, [product("V", 2, "a", (0, 1, 2)), product("V", 3, "a", (3,)), ("p_a", ne)], ("SY", "SY"))
+    finish("b", T.pos_b, [product("A", 4, "b", (0, 1)), product("V", 5, "b", (2,)), product("V", 6, "b", (3,)), ("p_b", ne)],
+           ("SY", "A"))
+
+    wait("g", *[e for e in list(unwaited.items()) if e != e_y])
+    wait("g", ("sent", sent[0]), e_y)

@@ -8,7 +8,9 @@ F8 = "float8_e4m3fn_x4"
 L_AT = {"o": 0, "a": CAPP, "s": 2 * CAPP, "b": 3 * CAPP + PAD}
 L_ALL = 4 * CAPP + PAD
 M_ALL = SLOTS + PAD
-ROUTE = ({"a": 0, "b": 0}, {"a": None, "b": 1}, {"a": None, "b": 1}, {"a": None, "b": None})
+X_HEAD = 512
+ROUTE = (({"a": None, "b": 0}, {"a": 0, "b": 0}), ({"a": None, "b": 1},) * 2, ({"a": None, "b": 1},) * 2,
+         ({"a": None, "b": None},) * 2)
 
 SCRATCH = {
     "xs": ("sbuf", [128, 4 * R], "bfloat16"),
@@ -45,7 +47,7 @@ for _k in "sab":
     SCRATCH["ys" + _k] = ("sbuf", [128, S], "float32")
 for _k in range(8):
     SCRATCH["ps%d" % _k] = ("psum", [128, 512], "float32")
-ARR = (["sent", "h_pos", "h0", "h1", "h2", "p_a", "p_b"] + [_s + _k for _s in ("l_", "f_") for _k in "abo"]
+ARR = (["sent", "h_pos", "h0c", "h0p", "h1c", "h1p", "h2c", "h2p", "p_a", "p_b"] + [_s + _k for _s in ("l_", "f_") for _k in "abo"]
        + ["m_%s%d" % (_k, _i) for _k in "ab" for _i in range(4)])
 SEMAPHORES = ARR + ["e%d" % _k for _k in range(125)]
 
@@ -96,13 +98,13 @@ def helper_program(g, core, T, topo, r, h):
     k = "ab"[h]
     g.wait_ge(T.sem.h_pos, len(near) // 2)
     send((T.cores[p[k]], T["pos_" + k][:], T.hpos[:], "p_" + k, out))
-    for i, route in enumerate(ROUTE):
-        sides = [k for k in "ab" if route[k] == h]
-        if sides:
-            g.wait_ge(T.sem["h%d" % i], 2 * len(near))
-        for k in sides:
-            for land, src in zip(block(T["mc_" + k], T["mp_" + k], i), block(T.hc, T.hp, i)):
-                send((T.cores[p[k]], land, src, "m_%s%d" % (k, i), out))
+    for i in range(N):
+        for j, route in enumerate(ROUTE[i]):
+            if h in route.values():
+                g.wait_ge(T.sem["h%d%s" % (i, "cp"[j])], len(near if None in route.values() else topo.engines(home, core)))
+            for k in "ab":
+                if route[k] == h:
+                    send((T.cores[p[k]], block(T["mc_" + k], T["mp_" + k], i)[j], block(T.hc, T.hp, i)[j], "m_%s%d" % (k, i), out))
     g.wait_ge(T.sem.sent, sent[0])
 
 
@@ -150,31 +152,30 @@ def rank_program(g, core, T, topo):
     nh = ne // 2
     halves = {"a": far[:nh], "b": far[nh:]}
 
-    e_want, e_slot, e_own, e_x, e_w, e_of, e_y = (event(32), event(32), event(16), event(16), event(16), event(64), event(96))
+    e_want, e_slot, e_own, e_x, e_w, e_of, e_y = (event(32), event(32), event(16), event(32), event(16), event(64), event(96))
 
     def load(q, out, src, e):
         q.dma_start(out, src).then_inc(T.sem[e[0]], 16)
 
-    v_half = done(V.memset(T.half[:], 0.5))
     v_ol = done(V.memset(T.ol[:], 0))
+    v_half = done(V.memset(T.half[:], 0.5))
     for k, q in enumerate((SY, A)):
         load(q, T.wl[16 * k:16 * k + 16, :], T.want[:], e_want)
-        load(q, T.sl[16 * k:16 * k + 16, :], T.slot[:], e_slot)
+    load(SY, T.xs[:, 0:X_HEAD], T.x[:, 0:X_HEAD], e_x)
+    for k in range(2):
+        load(A, T.sl[16 * k:16 * k + 16, :], T.slot[:], e_slot)
     wait("SY", v_ol)
     load(SY, T.ol[0:1, :], T.own[:], e_own)
-    load(SY, T.xs[:], T.x[:], e_x)
+    load(SY, T.xs[:, X_HEAD:4 * R], T.x[:, X_HEAD:4 * R], e_x)
 
     g_so = done(g.iota(T.so[:], [[0, 2], [16, 16]], 0, 1, allow_small_or_imprecise_dtypes=True))
     wait("g", v_half)
     g_id = done(g.affine_select(T.ident[:], T.half[:], [[-1, 128]], AluOpType.is_equal, 0.0, 0, 1))
     v_z = done(V.memset(T.et[:], 0.0))
-    wait("V", g_id, v_z)
-    v_e = done(V.tensor_copy(T.et[:, 3:512:4], T.ident[:]))
-    wait("V", v_e)
-    v_qe = done(*[V.quantize_mx(T.ec[:, 128 * b:128 * b + 128], T.ep[:, 128 * b:128 * b + 128], T.et[:, 3 - b:515 - b])
-                  for b in range(4)])
     wait("A", v_half)
     a_flat = done(*[A.activation(T.flat[:, 128 * j:128 * j + 128], T.half[:], COPY, scale=0.0) for j in range(3)])
+    wait("A", g_id, v_z)
+    a_e = done(A.activation(T.et[:, 3:512:4], T.ident[:], COPY))
     a_pad = done(*[A.activation(T[k][:, 4 * CAPP:512], T.half[:], COPY, scale=0.0)
                    for k in ("ta", "tb", "to", "ts", "mt0", "mt1", "mt2", "mt3")])
 
@@ -185,8 +186,8 @@ def rank_program(g, core, T, topo):
     def wcols(k):
         return T.w16[:, 6 * peer[k]:6 * peer[k] + 6]
 
-    send(*[(to[k], T["ask_" + k][:], wcols(k), "l_" + k, halves[k]) for k in "ab"])
-    send((to["o"], T.ask_o[:], wcols("o"), "l_o", far))
+    for k in "abo":
+        send((to[k], T["ask_" + k][:], wcols(k), "l_" + k, far))
 
     v_p16 = event(4)
 
@@ -212,9 +213,13 @@ def rank_program(g, core, T, topo):
     send(*[(hands[h], T.hpos[:], T.pos16[:], "h_pos", near[h * len(near) // 2:(h + 1) * len(near) // 2]) for h in range(2)])
     wait("V", e_own, v_o, a_flat)
     v_sc = done(V.tensor_copy(T.flat[:].indirect(T.so16[:]), T.ol[:]))
+    wait("V", a_e)
+    v_qe = done(*[V.quantize_mx(T.ec[:, 128 * b:128 * b + 128], T.ep[:, 128 * b:128 * b + 128], T.et[:, 3 - b:515 - b])
+                  for b in range(4)])
     wait("SY", v_sc)
     for k in range(4):
         load(SY, T.ownf[16 * k:16 * k + 16, :], T.flat[0:1, :], e_of)
+    wait("SY", e_x)
     load(SY, T.ws[:], T.w[:], e_w)
 
     def xwin(t):
@@ -228,10 +233,11 @@ def rank_program(g, core, T, topo):
         return done(*calls)
 
     for q in ("V", "A"):
-        wait(q, e_x)
-    for k, n in (("a", nh), ("b", nh), ("o", ne)):
+        wait(q, e_x, v_w16)
+    e_s = gather(T.ts, wcols("s"))
+    for k in "abo":
         for q in ("V", "A"):
-            wait(q, ("l_" + k, n))
+            wait(q, ("l_" + k, ne))
         e = gather(T["t" + k], T["ask_" + k][:])
         wait("V", a_pad, e)
         e = done(V.quantize_mx(T["c" + k][:], T["p" + k][:], T["t" + k][:]))
@@ -239,12 +245,9 @@ def rank_program(g, core, T, topo):
         at = L_AT[k]
         send((to[k], u8(T.lc[:, at:at + CAPP]), u8(T["c" + k][:, 0:CAPP]), "f_" + k, far))
         send((to[k], T.lp[:, at:at + CAPP], T["p" + k][:, 0:CAPP], "f_" + k, far))
-    for q in ("V", "A"):
-        wait(q, v_w16)
-    e = gather(T.ts, wcols("s"))
     wait("V", e_of)
     v_own = done(*[V.tensor_scalar(T.own16[p:p + 64, :], T.ownf[0:64, :], 4, None, mult) for p in (0, 64)])
-    wait("V", e)
+    wait("V", e_s)
     at = L_AT["s"]
     v_qs = done(V.quantize_mx(T.lc[:, at:at + 128], T.lp[:, at:at + 128], T.ts[:]))
 
@@ -281,14 +284,14 @@ def rank_program(g, core, T, topo):
             wait("V", v_q[i - 1])
         v_q[i] = done(V.quantize_mx(T.mc[:, m0:m0 + 128], T.mp[:, m0:m0 + 128], T["mt%d" % i][:]))
         wait("g", v_q[i])
-        straight = [k for k in "ab" if ROUTE[i][k] is None]
-        via = sorted(set(ROUTE[i].values()) - {None})
         src = block(T.mc, T.mp, i)
         land = {k: block(T["mc_" + k], T["mp_" + k], i) for k in "ab"}
-        if via:
-            for j in range(2):
+        if i < N - 1:
+            for j, route in enumerate(ROUTE[i]):
+                straight = [k for k in "ab" if route[k] is None]
+                via = max(v for v in route.values() if v is not None)
                 send(*[(to[k], land[k][j], src[j], "m_%s%d" % (k, i), far) for k in straight],
-                     (hands[via[0]], block(T.hc, T.hp, i)[j], src[j], "h%d" % i, near))
+                     (hands[via], block(T.hc, T.hp, i)[j], src[j], "h%d%s" % (i, "cp"[j]), near if straight else far + near))
         else:
             send(*[(to[k], land[k][1], src[1], "m_%s%d" % (k, i), halves[k]) for k in "ab"])
             for k in "ab":
@@ -321,9 +324,9 @@ def rank_program(g, core, T, topo):
 
     wait("PE", v_qw, *v_q.values())
     finish("s", T.pos16, [product("A", 0, "s", (0, 1)), product("V", 1, "s", (2, 3)), v_p16], ("SY", "SY"))
-    finish("a", T.pos_a, [product("V", 2, "a", (0, 1, 2)), product("V", 3, "a", (3,)), ("p_a", ne)], ("SY", "SY"))
-    finish("b", T.pos_b, [product("A", 4, "b", (0, 1)), product("V", 5, "b", (2,)), product("V", 6, "b", (3,)), ("p_b", ne)],
-           ("SY", "A"))
+    early = {"a": product("V", 2, "a", (0, 1, 2)), "b": product("A", 3, "b", (0, 1))}
+    finish("a", T.pos_a, [early["a"], product("V", 4, "a", (3,)), ("p_a", ne)], ("SY", "SY"))
+    finish("b", T.pos_b, [early["b"], product("A", 5, "b", (2,)), product("V", 6, "b", (3,)), ("p_b", ne)], ("SY", "A"))
 
     wait("g", *[e for e in list(unwaited.items()) if e != e_y])
     wait("g", ("sent", sent[0]), e_y)

from concourse.bass import DstId, RemoteDMATransfer
from concourse.mybir import dt, AluOpType, ActivationFunctionType

N, S, CAPP, R = 4, 256, 96, 1024
SLOTS = N * CAPP
PAD = 128 - CAPP
F8 = "float8_e4m3fn_x4"
L_AT = {"o": 0, "a": CAPP, "s": 2 * CAPP, "b": 3 * CAPP + PAD}
L_ALL = 4 * CAPP + PAD
M_ALL = SLOTS + PAD
X_HEAD = 512
ROUTE = (({"a": None, "b": 0}, {"a": 0, "b": 0}), ({"a": None, "b": 1},) * 2, ({"a": None, "b": 1},) * 2,
         ({"a": None, "b": None},) * 2)

SCRATCH = {
    "xs": ("sbuf", [128, 4 * R], "bfloat16"),
    "ws": ("sbuf", [128, 512], "bfloat16"),
    "wl": ("sbuf", [128, 24], "int32"), "sl": ("sbuf", [128, 16], "int32"), "ol": ("sbuf", [128, 256], "int32"),
    "w16": ("sbuf", [128, 24], "uint16"),
    "u1": ("sbuf", [128, 16], "int32"), "u2": ("sbuf", [128, 16], "int32"), "u3": ("sbuf", [128, 16], "int32"),
    "pos16": ("sbuf", [128, 16], "uint16"), "hpos": ("sbuf", [128, 16], "uint16"),
    "so": ("sbuf", [128, 32], "float32"), "sot": ("sbuf", [128, 32], "float32"), "so16": ("sbuf", [128, 16], "uint16"),
    "flat": ("sbuf", [128, SLOTS], "float32"), "ownf": ("sbuf", [128, 24], "float32"), "own16": ("sbuf", [128, 24], "uint16"),
    "half": ("sbuf", [128, 128], "bfloat16"), "ident": ("sbuf", [128, 128], "bfloat16"),
    "et": ("sbuf", [128, 516], "bfloat16"), "ec": ("sbuf", [128, 512], F8), "ep": ("sbuf", [128, 512], "uint8"),
    "wc": ("sbuf", [128, 128], F8), "wp": ("sbuf", [128, 128], "uint8"),
    "ts": ("sbuf", [128, 512], "bfloat16"),
    "lc": ("sbuf", [128, L_ALL], F8), "lp": ("sbuf", [128, L_ALL], "uint8"),
    "mc": ("sbuf", [128, M_ALL], F8), "mp": ("sbuf", [128, M_ALL], "uint8"),
    "hc": ("sbuf", [128, SLOTS], F8), "hp": ("sbuf", [128, SLOTS], "uint8"),
}
for _k in "abo":
    SCRATCH["ask_" + _k] = ("sbuf", [128, 6], "uint16")
    SCRATCH["t" + _k] = ("sbuf", [128, 512], "bfloat16")
    SCRATCH["c" + _k] = ("sbuf", [128, 128], F8)
    SCRATCH["p" + _k] = ("sbuf", [128, 128], "uint8")
for _k in "ab":
    SCRATCH["mc_" + _k] = ("sbuf", [128, SLOTS], F8)
    SCRATCH["mp_" + _k] = ("sbuf", [128, SLOTS], "uint8")
    SCRATCH["pos_" + _k] = ("sbuf", [128, 16], "uint16")
for _k in range(2):
    SCRATCH["xh%d" % _k] = ("sbuf", [128, 8 * CAPP], "bfloat16")
for _k in range(4):
    SCRATCH["mt%d" % _k] = ("sbuf", [128, 512], "bfloat16")
for _k in "sab":
    SCRATCH["yw" + _k] = ("sbuf", [128, SLOTS], "float32")
    SCRATCH["ys" + _k] = ("sbuf", [128, S], "float32")
for _k in range(8):
    SCRATCH["ps%d" % _k] = ("psum", [128, 512], "float32")
ARR = (["sent", "h_pos", "h0c", "h0p", "h1c", "h1p", "h2c", "h2p", "p_a", "p_b"] + [_s + _k for _s in ("l_", "f_") for _k in "abo"]
       + ["m_%s%d" % (_k, _i) for _k in "ab" for _i in range(4)])
SEMAPHORES = ARR + ["e%d" % _k for _k in range(125)]


def peers(r):
    a = r ^ 1
    return {"s": r, "a": a, "b": (2 * r - a) % N, "o": (r + 2) % N}


def helpers(T, topo, r):
    home, p = T.cores[r], peers(r)
    return [c for c in topo.cores_of(home) if topo.die(c) != topo.die(home)
            and all(topo.may_write(c, T.cores[p[k]]) for k in "ab")][:2]


def u8(v):
    return v.bitcast(dt.uint8)


def block(codes, plane, i):
    return u8(codes[:, CAPP * i:CAPP * i + CAPP]), plane[:, CAPP * i:CAPP * i + CAPP]


def writer(g, core, T, topo):
    sent = [0]

    def send(*items):
        tr = []
        for to, out, src, sem, es in items:
            rid, pid, _ = topo.addr(to)
            sent[0] += len(es)
            mask = sum(1 << e for e in es)
            if len(items) == 1:
                g.remote_dma(out_ap=out, in_ap=src, remote_sem=T.sem[sem], local_sem=T.sem.sent, pid=pid, routing_id=rid,
                             dma_engine_mask=mask)
                return
            tr.append(RemoteDMATransfer(dst_ids=[DstId(rid=rid, pnc=pid)], dma_engine_mask=mask,
                                        remote_sem=T.sem[sem], srcs=[src], dsts=[out]))
        g.remote_dma_fused(tr, local_sem=T.sem.sent)
    return send, sent


def helper_program(g, core, T, topo, r, h):
    send, sent = writer(g, core, T, topo)
    home, p = T.cores[r], peers(r)
    out = topo.engines(core, T.cores[p["a"]])
    near = [e for e in topo.engines(home, core) if e not in topo.engines(home, T.cores[p["a"]])]
    k = "ab"[h]
    g.wait_ge(T.sem.h_pos, len(near) // 2)
    send((T.cores[p[k]], T["pos_" + k][:], T.hpos[:], "p_" + k, out))
    for i in range(N):
        for j, route in enumerate(ROUTE[i]):
            if h in route.values():
                g.wait_ge(T.sem["h%d%s" % (i, "cp"[j])], len(near if None in route.values() else topo.engines(home, core)))
            for k in "ab":
                if route[k] == h:
                    send((T.cores[p[k]], block(T["mc_" + k], T["mp_" + k], i)[j], block(T.hc, T.hp, i)[j], "m_%s%d" % (k, i), out))
    g.wait_ge(T.sem.sent, sent[0])


def rank_program(g, core, T, topo):
    r = T.rank_of(core)
    if r is None:
        for q in range(N):
            if core in helpers(T, topo, q):
                helper_program(g, core, T, topo, q, helpers(T, topo, q).index(core))
        return
    V, A, PE, SY = g.vector, g.scalar, g.tensor, g.sync
    queues = {"g": g, "V": V, "A": A, "PE": PE, "SY": SY}
    add, mult = AluOpType.add, AluOpType.mult
    COPY = ActivationFunctionType.Copy
    peer = peers(r)
    to = {k: T.cores[peer[k]] for k in "abo"}
    hands = helpers(T, topo, r)
    nevents = [0]
    seen = set()
    unwaited = {}

    def event(n=1):
        name = "e%d" % nevents[0]
        nevents[0] += 1
        unwaited[name] = n
        return (name, n)

    def wait(q, *evs):
        for name, n in evs:
            if (q, name) not in seen:
                seen.add((q, name))
                unwaited.pop(name, None)
                queues[q].wait_ge(T.sem[name], n)

    def done(*calls):
        e = event(len(calls))
        for ins in calls:
            ins.then_inc(T.sem[e[0]], 1)
        return e

    send, sent = writer(g, core, T, topo)
    far = topo.engines(core, to["a"])
    near = [e for e in topo.engines(core, hands[0]) if e not in far]
    ne = len(far)
    nh = ne // 2
    halves = {"a": far[:nh], "b": far[nh:]}

    e_want, e_slot, e_own, e_x, e_w, e_of, e_y = (event(32), event(32), event(16), event(32), event(16), event(64), event(96))

    def load(q, out, src, e):
        q.dma_start(out, src).then_inc(T.sem[e[0]], 16)

    v_ol = done(V.memset(T.ol[:], 0))
    v_half = done(V.memset(T.half[:], 0.5))
    for k, q in enumerate((SY, A)):
        load(q, T.wl[16 * k:16 * k + 16, :], T.want[:], e_want)
    load(SY, T.xs[:, 0:X_HEAD], T.x[:, 0:X_HEAD], e_x)
    for k in range(2):
        load(A, T.sl[16 * k:16 * k + 16, :], T.slot[:], e_slot)
    wait("SY", v_ol)
    load(SY, T.ol[0:1, :], T.own[:], e_own)
    load(SY, T.xs[:, X_HEAD:4 * R], T.x[:, X_HEAD:4 * R], e_x)

    g_so = done(g.iota(T.so[:], [[0, 2], [16, 16]], 0, 1, allow_small_or_imprecise_dtypes=True))
    wait("g", v_half)
    g_id = done(g.affine_select(T.ident[:], T.half[:], [[-1, 128]], AluOpType.is_equal, 0.0, 0, 1))
    v_z = done(V.memset(T.et[:], 0.0))
    wait("A", v_half)
    a_flat = done(*[A.activation(T.flat[:, 128 * j:128 * j + 128], T.half[:], COPY, scale=0.0) for j in range(3)])
    wait("A", g_id, v_z)
    a_e = done(A.activation(T.et[:, 3:512:4], T.ident[:], COPY))
    a_pad = done(*[A.activation(T[k][:, 4 * CAPP:512], T.half[:], COPY, scale=0.0)
                   for k in ("ta", "tb", "to", "ts", "mt0", "mt1", "mt2", "mt3")])

    wait("V", e_want)
    v_w16 = done(*[V.tensor_scalar(T.w16[p:p + 32, :], T.wl[0:32, :], 0, 4, AluOpType.max, mult) for p in range(0, 128, 32)])
    wait("g", v_w16)

    def wcols(k):
        return T.w16[:, 6 * peer[k]:6 * peer[k] + 6]

    for k in "abo":
        send((to[k], T["ask_" + k][:], wcols(k), "l_" + k, far))

    v_p16 = event(4)

    def positions(p):
        V.tensor_copy(T.pos16[p:p + 32, :], T.sl[0:32, :]).then_inc(T.sem[v_p16[0]], 1)

    wait("V", e_slot)
    v1 = done(V.tensor_scalar(T.u1[0:16, :], T.sl[0:16, :], 4, None, AluOpType.arith_shift_right))
    v2 = done(V.tensor_scalar(T.u2[0:16, :], T.sl[0:16, :], 24, None, mult))
    wait("V", v1)
    v3 = done(V.tensor_scalar(T.u3[0:16, :], T.u1[0:16, :], 1 - SLOTS, None, mult))
    positions(0)
    wait("V", v2, v3, g_so)
    v_s = done(V.tensor_tensor(T.so[0:16, 0:16], T.u2[0:16, :], T.u3[0:16, :], add))
    positions(32)
    wait("V", v_s)
    v_t = done(V.transpose(T.sot[:], T.so[:]))
    positions(64)
    wait("V", v_t)
    v_o = done(V.tensor_copy(T.so16[:], T.sot[:, 0:16]))
    positions(96)
    wait("g", v_p16)
    send(*[(hands[h], T.hpos[:], T.pos16[:], "h_pos", near[h * len(near) // 2:(h + 1) * len(near) // 2]) for h in range(2)])
    wait("V", e_own, v_o, a_flat)
    v_sc = done(V.tensor_copy(T.flat[:].indirect(T.so16[:]), T.ol[:]))
    wait("V", a_e)
    v_qe = done(*[V.quantize_mx(T.ec[:, 128 * b:128 * b + 128], T.ep[:, 128 * b:128 * b + 128], T.et[:, 3 - b:515 - b])
                  for b in range(4)])
    wait("SY", v_sc)
    for k in range(4):
        load(SY, T.ownf[16 * k:16 * k + 16, :], T.flat[0:1, :], e_of)
    wait("SY", e_x)
    load(SY, T.ws[:], T.w[:], e_w)

    def xwin(t):
        return T.xs[:, t:4 * R]

    def gather(tile, off):
        calls = []
        for t in range(4):
            out, src = tile[:, t:4 * CAPP:4], xwin(t).indirect(off)
            calls.append(V.tensor_copy(out, src) if t < 2 else A.activation(out, src, COPY))
        return done(*calls)

    for q in ("V", "A"):
        wait(q, e_x, v_w16)
    e_s = gather(T.ts, wcols("s"))
    for k in "abo":
        for q in ("V", "A"):
            wait(q, ("l_" + k, ne))
        e = gather(T["t" + k], T["ask_" + k][:])
        wait("V", a_pad, e)
        e = done(V.quantize_mx(T["c" + k][:], T["p" + k][:], T["t" + k][:]))
        wait("g", e)
        at = L_AT[k]
        send((to[k], u8(T.lc[:, at:at + CAPP]), u8(T["c" + k][:, 0:CAPP]), "f_" + k, far))
        send((to[k], T.lp[:, at:at + CAPP], T["p" + k][:, 0:CAPP], "f_" + k, far))
    wait("V", e_of)
    v_own = done(*[V.tensor_scalar(T.own16[p:p + 64, :], T.ownf[0:64, :], 4, None, mult) for p in (0, 64)])
    wait("V", e_s)
    at = L_AT["s"]
    v_qs = done(V.quantize_mx(T.lc[:, at:at + 128], T.lp[:, at:at + 128], T.ts[:]))

    for q in ("V", "A"):
        wait(q, v_own)

    def own_columns(h, t, q):
        out, src = T["xh%d" % h][:, 2 * CAPP * t:2 * CAPP * t + 2 * CAPP], xwin(t).indirect(T.own16[:, 12 * h:12 * h + 12])
        return done(V.tensor_scalar(out, src, 0.5, None, mult) if q == "V" else A.activation(out, src, COPY, scale=0.5))

    ev_x = {r // 2: [own_columns(r // 2, t, "VVAA"[t]) for t in range(4)],
            1 - r // 2: [own_columns(1 - r // 2, t, "A") for t in range(4)]}

    v_m, v_q = {}, {}
    for i, k in enumerate("sabo"):
        q = peer[k]
        skip = PAD if k == "b" else 0
        at = L_AT[k] - skip
        bank, h, c = 4 * (i % 2), q // 2, CAPP * (q % 2)
        m0 = CAPP * i
        wait("PE", v_qe, ("f_" + k, 2 * ne) if i else v_qs)
        dec, v_m[i] = [], []
        for b in range(4):
            if i > 1:
                wait("PE", v_q[i - 2])
            dec.append(done(PE.matmul_mx(T["ps%d" % (bank + b)][:, 0:128], T.ec[:, 128 * b:128 * b + 128], T.ep[:, 128 * b:128 * b + 128],
                                         T.lc[:, at:at + 128], T.lp[:, at:at + 128], True, True)))
        for b in range(4):
            wait("V", dec[b], ev_x[h][b])
            v_m[i].append(V.tensor_tensor(T["mt%d" % i][:, b:4 * CAPP:4], T["ps%d" % (bank + b)][:, skip:skip + CAPP],
                                          T["xh%d" % h][:, 2 * CAPP * b + c:2 * CAPP * b + c + CAPP], add))
        wait("V", done(*v_m[i]))
        if i:
            wait("V", v_q[i - 1])
        v_q[i] = done(V.quantize_mx(T.mc[:, m0:m0 + 128], T.mp[:, m0:m0 + 128], T["mt%d" % i][:]))
        wait("g", v_q[i])
        src = block(T.mc, T.mp, i)
        land = {k: block(T["mc_" + k], T["mp_" + k], i) for k in "ab"}
        if i < N - 1:
            for j, route in enumerate(ROUTE[i]):
                straight = [k for k in "ab" if route[k] is None]
                via = max(v for v in route.values() if v is not None)
                send(*[(to[k], land[k][j], src[j], "m_%s%d" % (k, i), far) for k in straight],
                     (hands[via], block(T.hc, T.hp, i)[j], src[j], "h%d%s" % (i, "cp"[j]), near if straight else far + near))
        else:
            send(*[(to[k], land[k][1], src[1], "m_%s%d" % (k, i), halves[k]) for k in "ab"])
            for k in "ab":
                send((to[k], land[k][0], src[0], "m_%s%d" % (k, i), far))
    wait("V", e_w)
    v_qw = done(V.quantize_mx(T.wc[:], T.wp[:], T.ws[:]))

    def copy(q, out, src):
        return V.tensor_copy(out, src) if q == "V" else A.activation(out, src, COPY)

    def product(q, bank, k, blocks):
        codes, plane = (T.mc, T.mp) if k == "s" else (T["mc_" + k], T["mp_" + k])
        if k != "s":
            wait("PE", *[("m_%s%d" % (k, j), 2 * ne if j < 3 else ne + nh) for j in blocks])
        end = CAPP * blocks[-1] + CAPP
        first = min(CAPP * blocks[0], end - 128)
        ps = T["ps%d" % bank]
        wait(q, done(PE.matmul_mx(ps[:, 0:end - first], T.wc[:], T.wp[:], codes[:, first:end], plane[:, first:end], True, True)))
        order = [peers(peer[k])[j] for j in "sabo"]
        return done(*[copy(q, T["yw" + k][:, CAPP * order[j]:CAPP * order[j] + CAPP], ps[:, CAPP * j - first:CAPP * j - first + CAPP])
                      for j in blocks])

    def finish(k, off, ready, stores):
        at = S * ((peer[k] - r + 1) % N)
        for q, a, sq in (("V", 0, stores[0]), ("A", 128, stores[1])):
            wait(q, *ready)
            e = done(copy(q, T["ys" + k][:, a:a + 128], T["yw" + k][:].indirect(off[:, a // 16:a // 16 + 8])))
            wait(sq, e)
            load(queues[sq], T.y[:, at + a:at + a + 128], T["ys" + k][:, a:a + 128], e_y)

    wait("PE", v_qw, *v_q.values())
    finish("s", T.pos16, [product("A", 0, "s", (0, 1)), product("V", 1, "s", (2, 3)), v_p16], ("SY", "SY"))
    early = {"a": product("V", 2, "a", (0, 1, 2)), "b": product("A", 3, "b", (0, 1))}
    finish("a", T.pos_a, [early["a"], product("V", 4, "a", (3,)), ("p_a", ne)], ("SY", "SY"))
    finish("b", T.pos_b, [early["b"], product("A", 5, "b", (2,)), product("V", 6, "b", (3,)), ("p_b", ne)], ("SY", "A"))

    wait("g", *[e for e in list(unwaited.items()) if e != e_y])
    wait("g", ("sent", sent[0]), e_y)
